import numpy as np, ml_dtypes
CORES = [1,5,17,21,33,37,49,53]
N = 8
import mx_ref
BF = ml_dtypes.bfloat16
def entries(a):
    return np.ascontiguousarray(a.T).reshape(-1)
def table(e):
    return np.ascontiguousarray(np.reshape(e, (-1, 16)).T).astype(np.int32)
def cols(t, e):
    v = np.concatenate([t.reshape(128, -1, 4), np.zeros((128, 1, 4), BF)], axis=1)
    return np.ascontiguousarray(v[:, e]).reshape(128, -1)
def f(rng, *shape):
    return mx_ref.flush((rng.standard_normal(shape, dtype=np.float32) * np.exp2(rng.integers(-2, 3, shape[:-1] + (1,)))).astype(BF))
def wide(rng, *shape, cols=0):
    v = rng.standard_normal(shape, dtype=np.float32) * np.exp2(rng.integers(-12, 13, shape)).astype(np.float32)
    if cols: v *= np.repeat(np.exp2(rng.integers(-cols, cols + 1, shape[:-2] + (1, shape[-1] // 4))) * (rng.random(shape[:-2] + (1, shape[-1] // 4)) > 0.0625), 4, axis=-1).astype(np.float32)
    return mx_ref.flush(v.astype(BF))
T, B, NB, SUM = 512, 256, 3, 1088
SIDE = np.array([0, 0, 0, 0, 1, 1, 1, 1])
CAP = np.where(SIDE[:, None] == SIDE[None, :], 224, 48)
ST = np.cumsum(CAP, axis=1) - CAP
def lists(rng, alone=False, same=False, full=False, last=False):
    it, it2, ob, bag = np.full((N, SUM), -1), np.full((N, SUM), -1), np.full((N, SUM), -1), np.full((N, SUM), -1)
    one = rng.integers(0, T, N)
    none = rng.permutation(N) if alone else np.full(N, -1)
    for r in range(N):
        has = np.zeros((N, B), bool)
        free = np.where(np.arange(N) == none[r], 0, CAP[:, r])
        if full: has[:, rng.integers(0, B)] = True
        g = np.flatnonzero(~has.any(axis=0))
        has[rng.permutation(np.repeat(np.arange(N), free - has.sum(axis=1)))[:len(g)], g] = True
        for s in range(N):
            n = CAP[s, r]; h = has[s].sum()
            k = n if full else rng.integers(h, free[s] + 1)
            has[s, rng.permutation(np.flatnonzero(~has[s]))[:k - h]] = True
            j = np.flatnonzero(has[s]); c = rng.permutation(n)[:k]
            if last: j, c = j[::-1], np.sort(c)
            else: j = rng.permutation(j)
            u = np.full(k, one[s]) if same else rng.integers(0, T, k)
            v = (u + rng.integers(1, T, k)) % T if same else rng.integers(0, T, k)
            v = np.where(rng.random(k) < (1.0 if alone else 0.25), -1, v)
            it[s, ST[s, r] + c] = u; it2[s, ST[s, r] + c] = v; ob[s, ST[s, r] + c] = j; bag[r, ST[r, s] + c] = j
    return {"it": np.stack([table(e) for e in it]), "it2": np.stack([table(e) for e in it2]), "ob": np.stack([table(e) for e in ob]), "bag": np.stack([table(e) for e in bag])}
def setup_inputs(rng):
    return {"ex": f(rng, N, 128, 4 * T), "w": f(rng, N, 128, 512 * NB), **lists(rng)}
def setup_inputs_alone(rng):
    return {**setup_inputs(rng), **lists(rng, alone=True)}
def setup_inputs_full(rng):
    return {**setup_inputs(rng), **lists(rng, full=True)}
def setup_inputs_last(rng):
    return {**setup_inputs(rng), **lists(rng, last=True)}
def setup_inputs_same(rng):
    return {**setup_inputs(rng), **lists(rng, same=True)}
def setup_inputs_spread(rng):
    d = setup_inputs(rng); d["ex"] = wide(rng, N, 128, 4 * T, cols=6); return d
def check_inputs(d):
    b = []
    it, it2, ob, bag = [np.stack([entries(d[k][r]) for r in range(N)]) for k in ("it", "it2", "ob", "bag")]
    if it.min() < -1 or it.max() >= T: b.append("it")
    if it2.min() < -1 or it2.max() >= T: b.append("it2")
    if (it2[it < 0] != -1).any(): b.append("a second item in an empty slot")
    if ob.min() < -1 or ob.max() >= B: b.append("ob")
    if bag.min() < -1 or bag.max() >= B: b.append("bag")
    for r in range(N):
        for s in range(N):
            n = CAP[s, r]; u = it[s, ST[s, r]:ST[s, r] + n]; j = bag[r, ST[r, s]:ST[r, s] + n]
            if ((u < 0) != (j < 0)).any(): b.append("bag and it differ in their empty slots")
            if (ob[s, ST[s, r]:ST[s, r] + n] != j).any(): b.append("ob and bag differ")
            j = j[j >= 0]
            if len(set(j.tolist())) != len(j): b.append("a bag named twice")
        if not set(range(B)) <= set(bag[r].tolist()): b.append("a bag without parts")
    return b
def reference(ex, w, it, it2, ob, bag):
    y = np.zeros((N, 128, B * NB), np.float32)
    for r in range(N):
        W = [mx_ref.quantize(w[r][:, 512 * o:512 * o + 512]) for o in range(NB)]
        for s in range(N):
            n = CAP[s, r]
            u, v = entries(it[s])[ST[s, r]:ST[s, r] + n], entries(it2[s])[ST[s, r]:ST[s, r] + n]
            part = (cols(ex[s], u).astype(np.float32) + cols(ex[s], v).astype(np.float32)).astype(BF)
            P = mx_ref.quantize(part)
            j = entries(bag[r])[ST[r, s]:ST[r, s] + n]; used = j >= 0
            for o in range(NB): y[r][:, B * o + j[used]] += mx_ref.matmul(W[o], P)[:, used]
    return {"y": y}

@@ -1,0 +1,328 @@
+import numpy as np
+from concourse.bass import DstId, RemoteDMATransfer
+from concourse.mybir import dt, AluOpType, ActivationFunctionType
+
+N = 8
+SIDE = [0, 0, 0, 0, 1, 1, 1, 1]
+NEAR, FAR = 14, 3
+B, NB = 256, 3
+PAD = 16
+WIN = PAD + 2048
+XW = 864
+FW = 1696
+
+I32, F32, BF, U16, U8, Q8 = "int32", "float32", "bfloat16", "uint16", "uint8", "float8_e4m3fn_x4"
+SCRATCH = {
+    "EB": ("sbuf", [128, WIN], BF),
+    "WB": ("sbuf", [128, 1536], BF), "QW": ("sbuf", [128, 384], Q8), "SW": ("sbuf", [128, 384], U8),
+    "OBL": ("sbuf", [128, 14], I32), "UL": ("sbuf", [128, 7], I32), "VL": ("sbuf", [128, 7], I32),
+    "FL": ("sbuf", [128, 24], I32), "BD": ("dram", [16, 4, 12], I32), "BGL": ("sbuf", [128, 48], I32),
+    "TR": ("sbuf", [128, 14], I32), "TRF": ("sbuf", [128, 48], I32), "OC": ("sbuf", [128, 48], I32),
+    "IP": ("sbuf", [128, 2], I32),
+    "HI": ("sbuf", [128, 14], I32), "POS": ("sbuf", [128, 14], I32), "OFM": ("sbuf", [128, 14], I32),
+    "PI": ("sbuf", [128, 2], I32), "PF32": ("sbuf", [128, 2], F32),
+    "OFS": ("sbuf", [128, 14], U16),
+    "SC": ("sbuf", [128, 224], F32), "VAL": ("sbuf", [128, 224], F32),
+    "X": ("sbuf", [128, XW], F32), "XT": ("sbuf", [128, 512], F32),
+    "UV": ("sbuf", [128, 32], I32), "E8": ("sbuf", [128, 128], U16), "LUV": ("sbuf", [128, 512], U16),
+    "B1": ("sbuf", [128, 48], I32), "B2": ("sbuf", [128, 48], I32), "B3": ("sbuf", [128, 48], I32),
+    "LB": ("sbuf", [128, 48], U16),
+    "UF": ("sbuf", [128, 768], BF), "HF": ("sbuf", [128, 768], BF),
+    "QF": ("sbuf", [128, 192], Q8), "SF": ("sbuf", [128, 192], U8),
+    "RF": ("sbuf", [128, 192], Q8), "RFS": ("sbuf", [128, 192], U8),
+    "YF": ("sbuf", [128, 576], F32), "TMP": ("sbuf", [128, 576], F32), "F": ("sbuf", [128, FW], F32),
+    "YO": ("sbuf", [128, 768], F32),
+    "PN": ("psum", [128, 1536], F32), "PFAR": ("psum", [128, 1536], F32),
+}
+for _t in range(4):
+    SCRATCH["FUV%d" % _t] = ("sbuf", [128, 24], U16)
+for _a in range(4):
+    SCRATCH["UB%d" % _a] = ("sbuf", [128, 1024], BF)
+    SCRATCH["HB%d" % _a] = ("sbuf", [128, 1024], BF)
+    SCRATCH["Q%d" % _a] = ("sbuf", [128, 256], Q8)
+    SCRATCH["S%d" % _a] = ("sbuf", [128, 256], U8)
+for _a in range(3):
+    SCRATCH["R%d" % _a] = ("sbuf", [128, 256], Q8)
+    SCRATCH["RS%d" % _a] = ("sbuf", [128, 256], U8)
+EVENTS = 120
+SEMAPHORES = ["e%d" % i for i in range(EVENTS)] + ["sent", "farin", "in0", "in1", "in2"]
+
+
+def rank_program(g, core, T, topo):
+    me = T.rank_of(core)
+    if me is None:
+        return
+    v, s, sy, te = g.vector, g.scalar, g.sync, g.tensor
+    Op, Copy = AluOpType, ActivationFunctionType.Copy
+    cores = list(T.cores)
+
+    start, c = [], 0
+    for r in range(N):
+        start.append(c)
+        c += NEAR if SIDE[r] == SIDE[me] else FAR
+    far = [r for r in range(N) if SIDE[r] != SIDE[me]]
+    near = [r for r in range(N) if SIDE[r] == SIDE[me] and r != me]
+    fcol = start[far[0]]
+    same_chip = lambda r: topo.chip(cores[r]) == topo.chip(core)
+    same_die = lambda r: topo.die(cores[r]) == topo.die(core)
+    order = sorted(near, key=lambda r: (2 if same_chip(r) else 0) + (0 if same_die(r) else 1)) + [me]
+
+    made, seen = [0], {}
+
+    def ev():
+        e = ["e%d" % made[0], 0]
+        made[0] += 1
+        return e
+
+    def do(inst, e, n=1):
+        inst.then_inc(T.sem[e[0]], n)
+        e[1] += n
+
+    def wait(qn, q, *es):
+        for e in es:
+            if (qn, e[0]) not in seen:
+                seen[(qn, e[0])] = True
+                q.wait_ge(T.sem[e[0]], e[1])
+
+    e_ob, e_uv, e_ex, e_fl, e_w, e_bd, e_bag = ev(), ev(), ev(), ev(), ev(), ev(), ev()
+    for k in range(8):
+        c0 = start[order[k // 2]]
+        do((s if k % 2 else sy).dma_start(T.OBL[16 * k:16 * k + 16, :], T.ob[:, c0:c0 + 14]), e_ob, 16)
+    for k in range(8):
+        c0 = start[order[k // 2]] + 7 * (k % 2)
+        do(sy.dma_start(T.UL[16 * k:16 * k + 16, :], T.it[:, c0:c0 + 7]), e_uv, 16)
+        do(s.dma_start(T.VL[16 * k:16 * k + 16, :], T.it2[:, c0:c0 + 7]), e_uv, 16)
+    do(sy.dma_start(T.EB[:, PAD:WIN], T.ex[:, :]), e_ex, 16)
+    for k in range(8):
+        p = 16 * k
+        do(s.dma_start(T.FL[p:p + 16, 0:12], T.it[:, fcol:fcol + 12]), e_fl, 16)
+        do(sy.dma_start(T.FL[p:p + 16, 12:24], T.it2[:, fcol:fcol + 12]), e_fl, 16)
+    do(s.dma_start(T.WB[:, :], T.w[:, :]), e_w, 16)
+    for o in range(4):
+        do(sy.dma_start(T.BD[:, :, 3 * o:3 * o + 3], T.bag[:, fcol:fcol + 12]), e_bd, 16)
+    wait("sy", sy, e_bd)
+    for k in range(8):
+        do(sy.dma_start(T.BGL[16 * k:16 * k + 16, :], T.BD[:, :, :]), e_bag, 16)
+
+    e_ip, e_tr, e_trf, e_f = ev(), ev(), ev(), ev()
+    do(g.iota(T.IP[:, :], [[0, 2]], 0, 1), e_ip)
+    do(g.iota(T.TR[:, :], [[16, 14]], 512, 1), e_tr)
+    do(g.iota(T.TRF[:, :], [[0, 4], [256, 4], [16, 3]], 768, 1), e_trf)
+    do(g.iota(T.OC[:, :], [[0, 4], [256, 4], [0, 3]], 0, 0), e_trf)
+    do(g.iota(T.F[:, :], [[0, FW]], 0, 0, allow_small_or_imprecise_dtypes=True), e_f)
+    e_z, e_h0, e_h1 = ev(), ev(), ev()
+    do(v.memset(T.SC[:, :], 0.0), e_z)
+    do(v.memset(T.EB[:, 0:PAD], 0.0), e_z)
+    do(v.memset(T.X[:, 0:512], 0.0), e_z)
+    wait("v", v, e_ip)
+    do(v.tensor_scalar(T.PI[:, :], T.IP[:, :], 16, None, Op.bitwise_and), e_h0)
+    wait("v", v, e_h0)
+    do(v.tensor_copy(T.PF32[:, :], T.PI[:, :]), e_h1)
+
+    e1, e2, e3, e4, e5, e6 = ev(), ev(), ev(), ev(), ev(), ev()
+    e_sc, e_val = ev(), ev()
+    wait("v", v, e_ob)
+    do(v.tensor_scalar(T.HI[:, :], T.OBL[:, :], 0x3FF0, None, Op.bitwise_and), e1)
+    wait("v", v, e1)
+    do(v.tensor_tensor(T.POS[:, :], T.OBL[:, :], T.HI[:, :], Op.add), e2)
+    wait("v", v, e_uv, e_z)
+    do(v.tensor_scalar(T.SC[:, 0:224:32], T.UL[:, :], 4, 4, Op.mult, Op.add), e_sc)
+    do(v.tensor_scalar(T.SC[:, 16:224:32], T.UL[:, :], 4, 4, Op.mult, Op.add), e_sc)
+    wait("v", v, e2, e_tr)
+    do(v.tensor_tensor(T.OFM[:, :], T.POS[:, :], T.TR[:, :], Op.min), e3)
+    do(v.tensor_scalar(T.SC[:, 1:224:32], T.VL[:, :], 4, 4, Op.mult, Op.add), e_sc)
+    do(v.tensor_scalar(T.SC[:, 17:224:32], T.VL[:, :], 4, 4, Op.mult, Op.add), e_sc)
+    wait("v", v, e3, e_h1)
+    do(v.tensor_scalar(T.OFS[:, 0:14:2], T.OFM[:, 0:7], T.PF32[:, 0:1], None, Op.add), e4)
+    do(v.tensor_scalar(T.OFS[:, 1:14:2], T.OFM[:, 7:14], T.PF32[:, 0:1], None, Op.add), e4)
+    wait("v", v, e_sc)
+    do(v.transpose(T.VAL[:, :], T.SC[:, :]), e_val)
+    wait("v", v, e_val, e4)
+    do(v.tensor_copy(T.X[:, 0:XW].indirect(T.OFS[:, 0:14]), T.VAL[:, :]), e5)
+    wait("v", v, e5)
+    do(v.transpose(T.XT[:, :], T.X[:, 0:512]), e6)
+    wait("v", v, e_fl)
+    e_fuv = [ev() for t in range(4)]
+    for t in range(4):
+        do(v.tensor_scalar(T["FUV%d" % t][:, :], T.FL[:, :], 4, PAD + t, Op.mult, Op.add), e_fuv[t])
+    e_uv4, e_e80, e_e8 = ev(), ev(), ev()
+    wait("v", v, e6)
+    do(v.tensor_tensor(T.UV[:, 0:16], T.XT[:, 0:512:32], T.XT[:, 16:512:32], Op.add), e_uv4)
+    do(v.tensor_tensor(T.UV[:, 16:32], T.XT[:, 1:512:32], T.XT[:, 17:512:32], Op.add), e_uv4)
+    wait("v", v, e_uv4)
+    for t in range(4):
+        do(v.tensor_scalar(T.E8[:, 32 * t:32 * t + 32], T.UV[:, :], PAD - 4 + t, None, Op.add), e_e8 if t else e_e80)
+
+    e_uf = [ev() for t in range(4)]
+    wait("s", s, e_ex, e_z)
+    for t in range(4):
+        wait("s", s, e_fuv[t])
+        do(s.activation(T.UF[:, 192 * t:192 * t + 192], T.EB[:, 0:WIN].indirect(T["FUV%d" % t][:, 0:12]), Copy), e_uf[t])
+    e_off0, e_off = ev(), [ev() for a in range(4)]
+
+    def hand(q, qn, a, lo, hi, e):
+        wait(qn, q, e_e80)
+        if hi > 32:
+            wait(qn, q, e_e8)
+        for b in range(4):
+            do(q.dma_start(T.LUV[32 * b:32 * b + 32, 128 * a + lo:128 * a + hi], T.E8[32 * a:32 * a + 32, lo:hi]), e, 16)
+
+    hand(sy, "sy", 0, 0, 32, e_off0)
+    hand(sy, "sy", 0, 32, 128, e_off[0])
+    hand(sy, "sy", 1, 0, 128, e_off[1])
+    hand(s, "s", 2, 0, 128, e_off[2])
+    hand(s, "s", 3, 0, 128, e_off[3])
+    wait("v", v, e_ex)
+    e_hf, e_qf, e_qw = ev(), ev(), ev()
+    for t in range(4):
+        wait("v", v, e_uf[t])
+        do(v.tensor_tensor(T.HF[:, t:768:4], T.EB[:, 0:WIN].indirect(T["FUV%d" % t][:, 12:24]),
+                           T.UF[:, 192 * t:192 * t + 192], Op.add), e_hf)
+    wait("v", v, e_w)
+    do(v.quantize_mx(T.QW[:, 0:384], T.SW[:, 0:384], T.WB[:, 0:1536]), e_qw)
+    wait("v", v, e_hf)
+    do(v.quantize_mx(T.QF[:, 0:192], T.SF[:, 0:192], T.HF[:, 0:768]), e_qf)
+
+    e_b1, e_b2, e_b3, e_lb = ev(), ev(), ev(), ev()
+    wait("v", v, e_bag)
+    do(v.tensor_scalar(T.B1[:, :], T.BGL[:, :], 0x3FFF, None, Op.bitwise_and), e_b1)
+
+    def bags(i):
+        if i == 0:
+            wait("v", v, e_b1, e_trf)
+            do(v.tensor_tensor(T.B2[:, :], T.B1[:, :], T.OC[:, :], Op.add), e_b2)
+        elif i == 1:
+            wait("v", v, e_b2)
+            do(v.tensor_tensor(T.B3[:, :], T.B2[:, :], T.TRF[:, :], Op.min), e_b3)
+        elif i == 2:
+            wait("v", v, e_b3)
+            do(v.tensor_copy(T.LB[:, :], T.B3[:, :]), e_lb)
+
+    e_q, e_h = [ev() for a in range(4)], [ev() for a in range(4)]
+    e_u = [[ev() for t in range(4)] for a in range(4)]
+
+    def first(a):
+        for t in range(4):
+            lu = 128 * a + 32 * t
+            wait("s", s, e_off0 if a + t == 0 else e_off[a])
+            do(s.activation(T["UB%d" % a][:, 256 * t:256 * t + 256], T.EB[:, 0:WIN].indirect(T.LUV[:, lu:lu + 16]), Copy), e_u[a][t])
+
+    def second(a, t):
+        lu = 128 * a + 32 * t
+        wait("v", v, e_off0 if a + t == 0 else e_off[a])
+        wait("v", v, e_u[a][t])
+        do(v.tensor_tensor(T["HB%d" % a][:, t:1024:4], T.EB[:, 0:WIN].indirect(T.LUV[:, lu + 16:lu + 32]),
+                           T["UB%d" % a][:, 256 * t:256 * t + 256], Op.add), e_h[a])
+
+    def pack(a):
+        wait("v", v, e_h[a])
+        do(v.quantize_mx(T["Q%d" % a][:, 0:256], T["S%d" % a][:, 0:256], T["HB%d" % a][:, 0:1024]), e_q[a])
+
+    for a in range(3):
+        first(a)
+        for t in range(4):
+            second(a, t)
+            if a == 0:
+                bags(t)
+            elif t == 0:
+                pack(a - 1)
+
+    wait("te", te, e_qw)
+    te.wait_ge(T.sem.farin, 4 * 2 * 2)
+    e_pf = ev()
+    for o in range(NB):
+        do(te.matmul_mx(T.PFAR[:, 512 * o:512 * o + 192], T.QW[:, 128 * o:128 * o + 128], T.SW[:, 128 * o:128 * o + 128],
+                        T.RF[:, 0:192], T.RFS[:, 0:192], True, True), e_pf)
+    wait("s", s, e_pf)
+    e_yf = [ev() for k in range(4)]
+    for k in range(4):
+        for o in range(NB):
+            do(s.activation(T.YF[:, 144 * k + 48 * o:144 * k + 48 * o + 48],
+                            T.PFAR[:, 512 * o + 48 * k:512 * o + 48 * k + 48], Copy), e_yf[k])
+    first(3)
+
+    wait("v", v, e_lb, e_f)
+    e_sum, e_put = [ev() for k in range(4)], [ev() for k in range(4)]
+
+    def there(k):
+        return T.F[:, 0:FW].indirect(T.LB[:, 12 * k:12 * k + 9])
+
+    def add(k):
+        wait("v", v, e_yf[k], e_put[k - 1])
+        do(v.tensor_tensor(T.TMP[:, 144 * k:144 * k + 144], there(k), T.YF[:, 144 * k:144 * k + 144], Op.add), e_sum[k])
+
+    def put(k):
+        if k:
+            wait("v", v, e_sum[k])
+        else:
+            wait("v", v, e_yf[k])
+        do(v.tensor_copy(there(k), (T.TMP if k else T.YF)[:, 144 * k:144 * k + 144]), e_put[k])
+
+    put(0)
+    pack(2)
+    add(1)
+    second(3, 0)
+    put(1)
+    second(3, 1)
+    add(2)
+    second(3, 2)
+    put(2)
+    second(3, 3)
+    add(3)
+    pack(3)
+    put(3)
+
+    sent = 0
+    wait("g", g, e_qf)
+    mine = [r for r in range(N) if SIDE[r] == SIDE[me]].index(me)
+    for src, dst, wd in (("QF", "RF", 0), ("SF", "RFS", 1)):
+        tr = []
+        for k, r in enumerate(far):
+            rid, pid, _ = topo.addr(cores[r])
+            en = topo.engines(core, cores[r])
+            n = len(en) // 4
+            m = sum(1 << x for x in en[n * k:n * k + n])
+            sv, dv = T[src][:, 48 * k:48 * k + 48], T[dst][:, 48 * mine:48 * mine + 48]
+            if wd == 0:
+                sv, dv = sv.bitcast(dt.uint8), dv.bitcast(dt.uint8)
+            tr.append(RemoteDMATransfer(dst_ids=[DstId(rid=rid, pnc=pid)], dma_engine_mask=m, remote_sem=T.sem.farin,
+                                        srcs=[sv], dsts=[dv]))
+            sent += n
+        g.remote_dma_fused(tr, local_sem=T.sem.sent)
+    arrived = []
+    for a in range(3):
+        r = order[a]
+        rid, pid, _ = topo.addr(cores[r])
+        en = topo.engines(core, cores[r])[-8:]
+        m = sum(1 << x for x in en)
+        wait("g", g, e_q[a])
+        g.remote_dma(T["R%d" % a][:, 0:256].bitcast(dt.uint8), T["Q%d" % a][:, 0:256].bitcast(dt.uint8),
+                     T.sem["in%d" % a], T.sem.sent, pid, rid, m)
+        g.remote_dma(T["RS%d" % a][:, 0:256], T["S%d" % a][:, 0:256], T.sem["in%d" % a], T.sem.sent, pid, rid, m)
+        sent += 2 * len(en)
+        arrived.append(2 * len(en))
+
+    e_pn = [ev() for o in range(NB)]
+    for i, a in enumerate((0, 2, 1, 3)):
+        if a == 3:
+            wait("te", te, e_q[3])
+            qt, st = T.Q3, T.S3
+        else:
+            te.wait_ge(T.sem["in%d" % a], arrived[a])
+            qt, st = T["R%d" % a], T["RS%d" % a]
+        for o in range(NB):
+            inst = te.matmul_mx(T.PN[:, 512 * o:512 * o + 256], T.QW[:, 128 * o:128 * o + 128],
+                                T.SW[:, 128 * o:128 * o + 128], qt[:, 0:256], st[:, 0:256], i == 0, i == 3)
+            if i == 3:
+                do(inst, e_pn[o])
+
+    wait("v", v, e_put[3])
+    e_y = ev()
+    for o in range(NB):
+        e = ev()
+        wait("v", v, e_pn[o])
+        do(v.tensor_tensor(T.YO[:, B * o:B * o + B], T.PN[:, 512 * o:512 * o + B], T.F[:, B * o:B * o + B], Op.add), e)
+        wait("sy", sy, e)
+        do(sy.dma_start(T.y[:, B * o:B * o + B], T.YO[:, B * o:B * o + B]), e_y, 16)
+    wait("sy", sy, e_y)
+    g.wait_ge(T.sem.sent, sent)

@@ -8,29 +8,29 @@ NEAR, FAR = 14, 3
 B, NB = 256, 3
 PAD = 16
 WIN = PAD + 2048
-XW = 864
-FW = 1696
+XW = 592
+FS = 416
+FW = NB * FS
+OFFSET = 255
+CUTS = ((0, 64, 128, 192, 256), (0, 64, 128, 256), (0, 128, 256))
 
 I32, F32, BF, U16, U8, Q8 = "int32", "float32", "bfloat16", "uint16", "uint8", "float8_e4m3fn_x4"
 SCRATCH = {
     "EB": ("sbuf", [128, WIN], BF),
     "WB": ("sbuf", [128, 1536], BF), "QW": ("sbuf", [128, 384], Q8), "SW": ("sbuf", [128, 384], U8),
-    "OBL": ("sbuf", [128, 14], I32), "UL": ("sbuf", [128, 7], I32), "VL": ("sbuf", [128, 7], I32),
-    "FL": ("sbuf", [128, 24], I32), "BD": ("dram", [16, 4, 12], I32), "BGL": ("sbuf", [128, 48], I32),
-    "TR": ("sbuf", [128, 14], I32), "TRF": ("sbuf", [128, 48], I32), "OC": ("sbuf", [128, 48], I32),
-    "IP": ("sbuf", [128, 2], I32),
-    "HI": ("sbuf", [128, 14], I32), "POS": ("sbuf", [128, 14], I32), "OFM": ("sbuf", [128, 14], I32),
+    "OBL": ("sbuf", [128, 14], I32), "UVL": ("sbuf", [128, 14], I32),
+    "FL": ("sbuf", [128, 24], I32), "BGL": ("sbuf", [128, 12], I32),
+    "TR": ("sbuf", [128, 14], I32), "TRF": ("sbuf", [128, 12], I32),
+    "IP": ("sbuf", [128, 2], I32), "CI": ("sbuf", [128, 14], I32), "CO": ("sbuf", [128, 14], U16),
     "PI": ("sbuf", [128, 2], I32), "PF32": ("sbuf", [128, 2], F32),
-    "OFS": ("sbuf", [128, 14], U16),
-    "SC": ("sbuf", [128, 224], F32), "VAL": ("sbuf", [128, 224], F32),
-    "X": ("sbuf", [128, XW], F32), "XT": ("sbuf", [128, 512], F32),
-    "UV": ("sbuf", [128, 32], I32), "E8": ("sbuf", [128, 128], U16), "LUV": ("sbuf", [128, 512], U16),
-    "B1": ("sbuf", [128, 48], I32), "B2": ("sbuf", [128, 48], I32), "B3": ("sbuf", [128, 48], I32),
-    "LB": ("sbuf", [128, 48], U16),
-    "UF": ("sbuf", [128, 768], BF), "HF": ("sbuf", [128, 768], BF),
+    "LO": ("sbuf", [128, 14], I32), "OFM": ("sbuf", [128, 14], I32), "OFS": ("sbuf", [128, 14], U16),
+    "SC": ("sbuf", [128, 224], BF), "VAL": ("sbuf", [128, 224], BF), "X": ("sbuf", [128, XW], BF),
+    "E": ("sbuf", [128, 4, 4, 64], U16), "LUV": ("sbuf", [128, 512], U16),
+    "B1": ("sbuf", [128, 12], I32), "B2": ("sbuf", [128, 12], I32), "LB": ("sbuf", [128, 4, 10], U16),
+    "VB": ("sbuf", [128, 1024], BF), "UF": ("sbuf", [128, 768], BF), "HF": ("sbuf", [128, 768], BF),
     "QF": ("sbuf", [128, 192], Q8), "SF": ("sbuf", [128, 192], U8),
     "RF": ("sbuf", [128, 192], Q8), "RFS": ("sbuf", [128, 192], U8),
-    "YF": ("sbuf", [128, 576], F32), "TMP": ("sbuf", [128, 576], F32), "F": ("sbuf", [128, FW], F32),
+    "YF": ("sbuf", [128, 4, 144], F32), "TMP": ("sbuf", [128, 576], F32), "F": ("sbuf", [128, FW], F32),
     "YO": ("sbuf", [128, 768], F32),
     "PN": ("psum", [128, 1536], F32), "PFAR": ("psum", [128, 1536], F32),
 }
@@ -84,193 +84,165 @@ def rank_program(g, core, T, topo):
                 seen[(qn, e[0])] = True
                 q.wait_ge(T.sem[e[0]], e[1])
 
-    e_ob, e_uv, e_ex, e_fl, e_w, e_bd, e_bag = ev(), ev(), ev(), ev(), ev(), ev(), ev()
-    for k in range(8):
-        c0 = start[order[k // 2]]
-        do((s if k % 2 else sy).dma_start(T.OBL[16 * k:16 * k + 16, :], T.ob[:, c0:c0 + 14]), e_ob, 16)
-    for k in range(8):
-        c0 = start[order[k // 2]] + 7 * (k % 2)
-        do(sy.dma_start(T.UL[16 * k:16 * k + 16, :], T.it[:, c0:c0 + 7]), e_uv, 16)
-        do(s.dma_start(T.VL[16 * k:16 * k + 16, :], T.it2[:, c0:c0 + 7]), e_uv, 16)
+    e_m, e_ob, e_uv, e_ex, e_fl, e_w, e_bd, e_bag = ev(), ev(), ev(), ev(), ev(), ev(), ev(), ev()
+    do(v.memset(T.OBL[:, :], -1), e_m)
+
+    def items(a):
+        c0 = start[order[a]]
+        do(sy.dma_start(T.UVL[32 * a:32 * a + 32, 0:7], T.it[:, c0:c0 + 14]), e_uv, 16)
+        do(s.dma_start(T.UVL[32 * a:32 * a + 32, 7:14], T.it2[:, c0:c0 + 14]), e_uv, 16)
+
+    items(0)
+    wait("sy", sy, e_m)
+    wait("s", s, e_m)
+    for a in range(4):
+        c0 = start[order[a]]
+        do(sy.dma_start(T.OBL[32 * a:32 * a + 16, 0:7], T.ob[0:8, c0:c0 + 14]), e_ob, 16)
+        do(s.dma_start(T.OBL[32 * a:32 * a + 16, 7:14], T.ob[8:16, c0:c0 + 14]), e_ob, 16)
+    for a in range(1, 4):
+        items(a)
     do(sy.dma_start(T.EB[:, PAD:WIN], T.ex[:, :]), e_ex, 16)
     for k in range(8):
         p = 16 * k
         do(s.dma_start(T.FL[p:p + 16, 0:12], T.it[:, fcol:fcol + 12]), e_fl, 16)
         do(sy.dma_start(T.FL[p:p + 16, 12:24], T.it2[:, fcol:fcol + 12]), e_fl, 16)
     do(s.dma_start(T.WB[:, :], T.w[:, :]), e_w, 16)
-    for o in range(4):
-        do(sy.dma_start(T.BD[:, :, 3 * o:3 * o + 3], T.bag[:, fcol:fcol + 12]), e_bd, 16)
-    wait("sy", sy, e_bd)
     for k in range(8):
-        do(sy.dma_start(T.BGL[16 * k:16 * k + 16, :], T.BD[:, :, :]), e_bag, 16)
+        do((s if k % 2 else sy).dma_start(T.BGL[16 * k:16 * k + 16, :], T.bag[:, fcol:fcol + 12]), e_bag, 16)
 
     e_ip, e_tr, e_trf, e_f = ev(), ev(), ev(), ev()
     do(g.iota(T.IP[:, :], [[0, 2]], 0, 1), e_ip)
-    do(g.iota(T.TR[:, :], [[16, 14]], 512, 1), e_tr)
-    do(g.iota(T.TRF[:, :], [[0, 4], [256, 4], [16, 3]], 768, 1), e_trf)
-    do(g.iota(T.OC[:, :], [[0, 4], [256, 4], [0, 3]], 0, 0), e_trf)
+    do(g.iota(T.CI[:, :], [[1, 7], [0, 2]], 0, 0), e_ip)
+    do(g.iota(T.TR[:, :], [[16, 14]], B, 1), e_tr)
+    do(g.iota(T.TRF[:, :], [[0, 4], [16, 3]], B, 1), e_trf)
     do(g.iota(T.F[:, :], [[0, FW]], 0, 0, allow_small_or_imprecise_dtypes=True), e_f)
-    e_z, e_h0, e_h1 = ev(), ev(), ev()
-    do(v.memset(T.SC[:, :], 0.0), e_z)
+    e_z, e_h0, e_h1, e_co = ev(), ev(), ev(), ev()
     do(v.memset(T.EB[:, 0:PAD], 0.0), e_z)
-    do(v.memset(T.X[:, 0:512], 0.0), e_z)
+    do(v.memset(T.X[:, 0:B], -1.0 - OFFSET), e_z)
     wait("v", v, e_ip)
-    do(v.tensor_scalar(T.PI[:, :], T.IP[:, :], 16, None, Op.bitwise_and), e_h0)
+    do(v.tensor_scalar(T.PI[:, :], T.IP[:, :], 8, None, Op.bitwise_and), e_h0)
     wait("v", v, e_h0)
-    do(v.tensor_copy(T.PF32[:, :], T.PI[:, :]), e_h1)
+    do(v.tensor_scalar(T.PF32[:, :], T.PI[:, :], 0.875, None, Op.mult), e_h1)
+    wait("v", v, e_h1)
+    do(v.tensor_scalar(T.CO[:, :], T.CI[:, :], T.PF32[:, 0:1], None, Op.add), e_co)
 
     e1, e2, e3, e4, e5, e6 = ev(), ev(), ev(), ev(), ev(), ev()
-    e_sc, e_val = ev(), ev()
+    e_sc, e_val, e_e = ev(), ev(), ev()
     wait("v", v, e_ob)
-    do(v.tensor_scalar(T.HI[:, :], T.OBL[:, :], 0x3FF0, None, Op.bitwise_and), e1)
-    wait("v", v, e1)
-    do(v.tensor_tensor(T.POS[:, :], T.OBL[:, :], T.HI[:, :], Op.add), e2)
-    wait("v", v, e_uv, e_z)
-    do(v.tensor_scalar(T.SC[:, 0:224:32], T.UL[:, :], 4, 4, Op.mult, Op.add), e_sc)
-    do(v.tensor_scalar(T.SC[:, 16:224:32], T.UL[:, :], 4, 4, Op.mult, Op.add), e_sc)
-    wait("v", v, e2, e_tr)
-    do(v.tensor_tensor(T.OFM[:, :], T.POS[:, :], T.TR[:, :], Op.min), e3)
-    do(v.tensor_scalar(T.SC[:, 1:224:32], T.VL[:, :], 4, 4, Op.mult, Op.add), e_sc)
-    do(v.tensor_scalar(T.SC[:, 17:224:32], T.VL[:, :], 4, 4, Op.mult, Op.add), e_sc)
-    wait("v", v, e3, e_h1)
-    do(v.tensor_scalar(T.OFS[:, 0:14:2], T.OFM[:, 0:7], T.PF32[:, 0:1], None, Op.add), e4)
-    do(v.tensor_scalar(T.OFS[:, 1:14:2], T.OFM[:, 7:14], T.PF32[:, 0:1], None, Op.add), e4)
+    do(v.tensor_scalar(T.LO[:, :], T.OBL[:, :], 0x3FF, None, Op.bitwise_and), e1)
+    wait("v", v, e_uv, e_z, e_co)
+    do(v.tensor_scalar(T.SC[:, :], T.UVL[:, 0:14].indirect(T.CO[:, 0:14]), -OFFSET, None, Op.add), e_sc)
+    wait("v", v, e1, e_tr)
+    do(v.tensor_tensor(T.OFM[:, :], T.LO[:, :], T.TR[:, :], Op.min), e4)
     wait("v", v, e_sc)
     do(v.transpose(T.VAL[:, :], T.SC[:, :]), e_val)
-    wait("v", v, e_val, e4)
-    do(v.tensor_copy(T.X[:, 0:XW].indirect(T.OFS[:, 0:14]), T.VAL[:, :]), e5)
-    wait("v", v, e5)
-    do(v.transpose(T.XT[:, :], T.X[:, 0:512]), e6)
-    wait("v", v, e_fl)
+    wait("v", v, e4)
+    do(v.tensor_copy(T.OFS[:, 0:14:2], T.OFM[:, 0:7]), e5)
+    do(v.tensor_copy(T.OFS[:, 1:14:2], T.OFM[:, 7:14]), e5)
+    wait("v", v, e_val, e5)
+    do(v.tensor_copy(T.X[:, 0:XW].indirect(T.OFS[:, 0:14]), T.VAL[:, :]), e6)
     e_fuv = [ev() for t in range(4)]
+    wait("v", v, e_fl)
     for t in range(4):
         do(v.tensor_scalar(T["FUV%d" % t][:, :], T.FL[:, :], 4, PAD + t, Op.mult, Op.add), e_fuv[t])
-    e_uv4, e_e80, e_e8 = ev(), ev(), ev()
     wait("v", v, e6)
-    do(v.tensor_tensor(T.UV[:, 0:16], T.XT[:, 0:512:32], T.XT[:, 16:512:32], Op.add), e_uv4)
-    do(v.tensor_tensor(T.UV[:, 16:32], T.XT[:, 1:512:32], T.XT[:, 17:512:32], Op.add), e_uv4)
-    wait("v", v, e_uv4)
     for t in range(4):
-        do(v.tensor_scalar(T.E8[:, 32 * t:32 * t + 32], T.UV[:, :], PAD - 4 + t, None, Op.add), e_e8 if t else e_e80)
+        do(v.tensor_scalar(T.E[:, :, t, :], T.X[:, 0:B], 4, 4 * OFFSET + PAD + t, Op.mult, Op.add), e_e)
+
+    e_tu, e_tv = [ev() for a in range(4)], [ev() for a in range(4)]
+    wait("sy", sy, e_e)
+    for a in range(4):
+        do(sy.dma_start(T.LUV[:, 128 * a:128 * a + 64], T.E[32 * a:32 * a + 8, :, :, :]), e_tu[a], 16)
+        do(sy.dma_start(T.LUV[:, 128 * a + 64:128 * a + 128], T.E[32 * a + 8:32 * a + 16, :, :, :]), e_tv[a], 16)
 
     e_uf = [ev() for t in range(4)]
     wait("s", s, e_ex, e_z)
     for t in range(4):
         wait("s", s, e_fuv[t])
         do(s.activation(T.UF[:, 192 * t:192 * t + 192], T.EB[:, 0:WIN].indirect(T["FUV%d" % t][:, 0:12]), Copy), e_uf[t])
-    e_off0, e_off = ev(), [ev() for a in range(4)]
-
-    def hand(q, qn, a, lo, hi, e):
-        wait(qn, q, e_e80)
-        if hi > 32:
-            wait(qn, q, e_e8)
-        for b in range(4):
-            do(q.dma_start(T.LUV[32 * b:32 * b + 32, 128 * a + lo:128 * a + hi], T.E8[32 * a:32 * a + 32, lo:hi]), e, 16)
-
-    hand(sy, "sy", 0, 0, 32, e_off0)
-    hand(sy, "sy", 0, 32, 128, e_off[0])
-    hand(sy, "sy", 1, 0, 128, e_off[1])
-    hand(s, "s", 2, 0, 128, e_off[2])
-    hand(s, "s", 3, 0, 128, e_off[3])
     wait("v", v, e_ex)
     e_hf, e_qf, e_qw = ev(), ev(), ev()
+    e_b1, e_b2, e_lb = ev(), ev(), ev()
     for t in range(4):
         wait("v", v, e_uf[t])
         do(v.tensor_tensor(T.HF[:, t:768:4], T.EB[:, 0:WIN].indirect(T["FUV%d" % t][:, 12:24]),
                            T.UF[:, 192 * t:192 * t + 192], Op.add), e_hf)
-    wait("v", v, e_w)
-    do(v.quantize_mx(T.QW[:, 0:384], T.SW[:, 0:384], T.WB[:, 0:1536]), e_qw)
+        if t == 1:
+            wait("v", v, e_bag)
+            do(v.tensor_scalar(T.B1[:, :], T.BGL[:, :], 0x3FF, None, Op.bitwise_and), e_b1)
+        if t == 2:
+            wait("v", v, e_b1, e_trf)
+            do(v.tensor_tensor(T.B2[:, :], T.B1[:, :], T.TRF[:, :], Op.min), e_b2)
+    wait("v", v, e_b2)
+    for o in range(NB):
+        do(v.tensor_scalar(T.LB[:, :, 3 * o:3 * o + 3], T.B2[:, :], FS * o, None, Op.add), e_lb)
     wait("v", v, e_hf)
     do(v.quantize_mx(T.QF[:, 0:192], T.SF[:, 0:192], T.HF[:, 0:768]), e_qf)
-
-    e_b1, e_b2, e_b3, e_lb = ev(), ev(), ev(), ev()
-    wait("v", v, e_bag)
-    do(v.tensor_scalar(T.B1[:, :], T.BGL[:, :], 0x3FFF, None, Op.bitwise_and), e_b1)
-
-    def bags(i):
-        if i == 0:
-            wait("v", v, e_b1, e_trf)
-            do(v.tensor_tensor(T.B2[:, :], T.B1[:, :], T.OC[:, :], Op.add), e_b2)
-        elif i == 1:
-            wait("v", v, e_b2)
-            do(v.tensor_tensor(T.B3[:, :], T.B2[:, :], T.TRF[:, :], Op.min), e_b3)
-        elif i == 2:
-            wait("v", v, e_b3)
-            do(v.tensor_copy(T.LB[:, :], T.B3[:, :]), e_lb)
+    wait("v", v, e_w)
+    do(v.quantize_mx(T.QW[:, 0:384], T.SW[:, 0:384], T.WB[:, 0:1536]), e_qw)
 
     e_q, e_h = [ev() for a in range(4)], [ev() for a in range(4)]
-    e_u = [[ev() for t in range(4)] for a in range(4)]
 
-    def first(a):
-        for t in range(4):
-            lu = 128 * a + 32 * t
-            wait("s", s, e_off0 if a + t == 0 else e_off[a])
-            do(s.activation(T["UB%d" % a][:, 256 * t:256 * t + 256], T.EB[:, 0:WIN].indirect(T.LUV[:, lu:lu + 16]), Copy), e_u[a][t])
+    def picked(a, second_item, lo, hi):
+        c0 = 128 * a + 64 * second_item
+        return T.EB[:, 0:WIN].indirect(T.LUV[:, c0 + lo // 4:c0 + hi // 4])
 
-    def second(a, t):
-        lu = 128 * a + 32 * t
-        wait("v", v, e_off0 if a + t == 0 else e_off[a])
-        wait("v", v, e_u[a][t])
-        do(v.tensor_tensor(T["HB%d" % a][:, t:1024:4], T.EB[:, 0:WIN].indirect(T.LUV[:, lu + 16:lu + 32]),
-                           T["UB%d" % a][:, 256 * t:256 * t + 256], Op.add), e_h[a])
+    def first(a, lo, hi, e):
+        wait("s", s, e_tu[a])
+        do(s.activation(T["UB%d" % a][:, 4 * lo:4 * hi], picked(a, 0, lo, hi), Copy), e)
 
-    def pack(a):
-        wait("v", v, e_h[a])
+    def second(a, lo, hi, e):
+        wait("v", v, e_tv[a], e)
+        do(v.tensor_tensor(T["HB%d" % a][:, 4 * lo:4 * hi], picked(a, 1, lo, hi), T["UB%d" % a][:, 4 * lo:4 * hi],
+                           Op.add), e_h[a])
+
+    def pack(a, *es):
+        wait("v", v, e_h[a], *es)
         do(v.quantize_mx(T["Q%d" % a][:, 0:256], T["S%d" % a][:, 0:256], T["HB%d" % a][:, 0:1024]), e_q[a])
 
     for a in range(3):
-        first(a)
-        for t in range(4):
-            second(a, t)
-            if a == 0:
-                bags(t)
-            elif t == 0:
+        for lo, hi in zip(CUTS[a], CUTS[a][1:]):
+            e = ev()
+            first(a, lo, hi, e)
+            second(a, lo, hi, e)
+            if a and lo == 0:
                 pack(a - 1)
 
     wait("te", te, e_qw)
     te.wait_ge(T.sem.farin, 4 * 2 * 2)
-    e_pf = ev()
+    e_pf, e_yf = [ev() for o in range(NB)], ev()
     for o in range(NB):
         do(te.matmul_mx(T.PFAR[:, 512 * o:512 * o + 192], T.QW[:, 128 * o:128 * o + 128], T.SW[:, 128 * o:128 * o + 128],
-                        T.RF[:, 0:192], T.RFS[:, 0:192], True, True), e_pf)
-    wait("s", s, e_pf)
-    e_yf = [ev() for k in range(4)]
-    for k in range(4):
-        for o in range(NB):
-            do(s.activation(T.YF[:, 144 * k + 48 * o:144 * k + 48 * o + 48],
-                            T.PFAR[:, 512 * o + 48 * k:512 * o + 48 * k + 48], Copy), e_yf[k])
-    first(3)
+                        T.RF[:, 0:192], T.RFS[:, 0:192], True, True), e_pf[o])
+    for o in range(NB):
+        wait("s", s, e_pf[o])
+        do(s.activation(T.YF[:, :, 48 * o:48 * o + 48], T.PFAR[:, 512 * o:512 * o + 192], Copy), e_yf)
+    e_u3 = [ev(), ev(), ev()]
+    first(3, 0, 128, e_u3[0])
+    wait("s", s, e_tv[3])
+    do(s.activation(T.VB[:, 256:512], picked(3, 1, 64, 128), Copy), e_u3[1])
+    first(3, 128, 256, e_u3[2])
+    do(s.activation(T.VB[:, 512:1024], picked(3, 1, 128, 256), Copy), e_u3[2])
 
     wait("v", v, e_lb, e_f)
     e_sum, e_put = [ev() for k in range(4)], [ev() for k in range(4)]
 
     def there(k):
-        return T.F[:, 0:FW].indirect(T.LB[:, 12 * k:12 * k + 9])
+        return T.F[:, 0:FW].indirect(T.LB[:, k, 0:9])
 
     def add(k):
-        wait("v", v, e_yf[k], e_put[k - 1])
-        do(v.tensor_tensor(T.TMP[:, 144 * k:144 * k + 144], there(k), T.YF[:, 144 * k:144 * k + 144], Op.add), e_sum[k])
+        wait("v", v, e_put[k - 1])
+        do(v.tensor_tensor(T.TMP[:, 144 * k:144 * k + 144], there(k), T.YF[:, k, :], Op.add), e_sum[k])
 
     def put(k):
-        if k:
-            wait("v", v, e_sum[k])
-        else:
-            wait("v", v, e_yf[k])
-        do(v.tensor_copy(there(k), (T.TMP if k else T.YF)[:, 144 * k:144 * k + 144]), e_put[k])
+        wait("v", v, e_sum[k] if k else e_yf)
+        do(v.tensor_copy(there(k), T.TMP[:, 144 * k:144 * k + 144] if k else T.YF[:, k, :]), e_put[k])
 
-    put(0)
-    pack(2)
-    add(1)
-    second(3, 0)
-    put(1)
-    second(3, 1)
-    add(2)
-    second(3, 2)
-    put(2)
-    second(3, 3)
-    add(3)
-    pack(3)
-    put(3)
+    def own(i):
+        if i == 0:
+            return second(3, 0, 64, e_u3[0])
+        wait("v", v, e_u3[min(i, 2)])
+        do(v.tensor_tensor(T.HB3[:, B * i:B * i + B], T.VB[:, B * i:B * i + B], T.UB3[:, B * i:B * i + B], Op.add), e_h[3])
 
     sent = 0
     wait("g", g, e_qf)
@@ -289,6 +261,9 @@ def rank_program(g, core, T, topo):
                                         srcs=[sv], dsts=[dv]))
             sent += n
         g.remote_dma_fused(tr, local_sem=T.sem.sent)
+
+    put(0)
+    pack(2)
     arrived = []
     for a in range(3):
         r = order[a]
@@ -301,6 +276,18 @@ def rank_program(g, core, T, topo):
         g.remote_dma(T["RS%d" % a][:, 0:256], T["S%d" % a][:, 0:256], T.sem["in%d" % a], T.sem.sent, pid, rid, m)
         sent += 2 * len(en)
         arrived.append(2 * len(en))
+
+    add(1)
+    own(0)
+    put(1)
+    own(1)
+    add(2)
+    own(2)
+    put(2)
+    own(3)
+    add(3)
+    pack(3)
+    put(3)
 
     e_pn = [ev() for o in range(NB)]
     for i, a in enumerate((0, 2, 1, 3)):
@@ -321,7 +308,9 @@ def rank_program(g, core, T, topo):
     for o in range(NB):
         e = ev()
         wait("v", v, e_pn[o])
-        do(v.tensor_tensor(T.YO[:, B * o:B * o + B], T.PN[:, 512 * o:512 * o + B], T.F[:, B * o:B * o + B], Op.add), e)
+        for i in range(4):
+            do(v.tensor_tensor(T.YO[:, B * o + 64 * i:B * o + 64 * i + 64], T.PN[:, 512 * o + i:512 * o + B:4],
+                               T.F[:, FS * o + 64 * i:FS * o + 64 * i + 64], Op.add), e)
         wait("sy", sy, e)
         do(sy.dma_start(T.y[:, B * o:B * o + B], T.YO[:, B * o:B * o + B]), e_y, 16)
     wait("sy", sy, e_y)

import numpy as np
from concourse.bass import DstId, RemoteDMATransfer
from concourse.mybir import dt, AluOpType, ActivationFunctionType

N = 8
SIDE = [0, 0, 0, 0, 1, 1, 1, 1]
NEAR, FAR = 14, 3
B, NB = 256, 3
PAD = 16
WIN = PAD + 2048
XW = 592
FS = 416
FW = NB * FS
OFFSET = 255
CUTS = ((0, 64, 128, 192, 256), (0, 64, 128, 256), (0, 128, 256))

I32, F32, BF, U16, U8, Q8 = "int32", "float32", "bfloat16", "uint16", "uint8", "float8_e4m3fn_x4"
SCRATCH = {
    "EB": ("sbuf", [128, WIN], BF),
    "WB": ("sbuf", [128, 1536], BF), "QW": ("sbuf", [128, 384], Q8), "SW": ("sbuf", [128, 384], U8),
    "OBL": ("sbuf", [128, 14], I32), "UVL": ("sbuf", [128, 14], I32),
    "FL": ("sbuf", [128, 24], I32), "BGL": ("sbuf", [128, 12], I32),
    "TR": ("sbuf", [128, 14], I32), "TRF": ("sbuf", [128, 12], I32),
    "IP": ("sbuf", [128, 2], I32), "CI": ("sbuf", [128, 14], I32), "CO": ("sbuf", [128, 14], U16),
    "PI": ("sbuf", [128, 2], I32), "PF32": ("sbuf", [128, 2], F32),
    "LO": ("sbuf", [128, 14], I32), "OFM": ("sbuf", [128, 14], I32), "OFS": ("sbuf", [128, 14], U16),
    "SC": ("sbuf", [128, 224], BF), "VAL": ("sbuf", [128, 224], BF), "X": ("sbuf", [128, XW], BF),
    "E": ("sbuf", [128, 4, 4, 64], U16), "LUV": ("sbuf", [128, 512], U16),
    "B1": ("sbuf", [128, 12], I32), "B2": ("sbuf", [128, 12], I32), "LB": ("sbuf", [128, 4, 10], U16),
    "VB": ("sbuf", [128, 1024], BF), "UF": ("sbuf", [128, 768], BF), "HF": ("sbuf", [128, 768], BF),
    "QF": ("sbuf", [128, 192], Q8), "SF": ("sbuf", [128, 192], U8),
    "RF": ("sbuf", [128, 192], Q8), "RFS": ("sbuf", [128, 192], U8),
    "YF": ("sbuf", [128, 4, 144], F32), "TMP": ("sbuf", [128, 576], F32), "F": ("sbuf", [128, FW], F32),
    "YO": ("sbuf", [128, 768], F32),
    "PN": ("psum", [128, 1536], F32), "PFAR": ("psum", [128, 1536], F32),
}
for _t in range(4):
    SCRATCH["FUV%d" % _t] = ("sbuf", [128, 24], U16)
for _a in range(4):
    SCRATCH["UB%d" % _a] = ("sbuf", [128, 1024], BF)
    SCRATCH["HB%d" % _a] = ("sbuf", [128, 1024], BF)
    SCRATCH["Q%d" % _a] = ("sbuf", [128, 256], Q8)
    SCRATCH["S%d" % _a] = ("sbuf", [128, 256], U8)
for _a in range(3):
    SCRATCH["R%d" % _a] = ("sbuf", [128, 256], Q8)
    SCRATCH["RS%d" % _a] = ("sbuf", [128, 256], U8)
EVENTS = 120
SEMAPHORES = ["e%d" % i for i in range(EVENTS)] + ["sent", "farin", "in0", "in1", "in2"]


def rank_program(g, core, T, topo):
    me = T.rank_of(core)
    if me is None:
        return
    v, s, sy, te = g.vector, g.scalar, g.sync, g.tensor
    Op, Copy = AluOpType, ActivationFunctionType.Copy
    cores = list(T.cores)

    start, c = [], 0
    for r in range(N):
        start.append(c)
        c += NEAR if SIDE[r] == SIDE[me] else FAR
    far = [r for r in range(N) if SIDE[r] != SIDE[me]]
    near = [r for r in range(N) if SIDE[r] == SIDE[me] and r != me]
    fcol = start[far[0]]
    same_chip = lambda r: topo.chip(cores[r]) == topo.chip(core)
    same_die = lambda r: topo.die(cores[r]) == topo.die(core)
    order = sorted(near, key=lambda r: (2 if same_chip(r) else 0) + (0 if same_die(r) else 1)) + [me]

    made, seen = [0], {}

    def ev():
        e = ["e%d" % made[0], 0]
        made[0] += 1
        return e

    def do(inst, e, n=1):
        inst.then_inc(T.sem[e[0]], n)
        e[1] += n

    def wait(qn, q, *es):
        for e in es:
            if (qn, e[0]) not in seen:
                seen[(qn, e[0])] = True
                q.wait_ge(T.sem[e[0]], e[1])

    e_m, e_ob, e_uv, e_ex, e_fl, e_w, e_bd, e_bag = ev(), ev(), ev(), ev(), ev(), ev(), ev(), ev()
    do(v.memset(T.OBL[:, :], -1), e_m)

    def items(a):
        c0 = start[order[a]]
        do(sy.dma_start(T.UVL[32 * a:32 * a + 32, 0:7], T.it[:, c0:c0 + 14]), e_uv, 16)
        do(s.dma_start(T.UVL[32 * a:32 * a + 32, 7:14], T.it2[:, c0:c0 + 14]), e_uv, 16)

    items(0)
    wait("sy", sy, e_m)
    wait("s", s, e_m)
    for a in range(4):
        c0 = start[order[a]]
        do(sy.dma_start(T.OBL[32 * a:32 * a + 16, 0:7], T.ob[0:8, c0:c0 + 14]), e_ob, 16)
        do(s.dma_start(T.OBL[32 * a:32 * a + 16, 7:14], T.ob[8:16, c0:c0 + 14]), e_ob, 16)
    for a in range(1, 4):
        items(a)
    do(sy.dma_start(T.EB[:, PAD:WIN], T.ex[:, :]), e_ex, 16)
    for k in range(8):
        p = 16 * k
        do(s.dma_start(T.FL[p:p + 16, 0:12], T.it[:, fcol:fcol + 12]), e_fl, 16)
        do(sy.dma_start(T.FL[p:p + 16, 12:24], T.it2[:, fcol:fcol + 12]), e_fl, 16)
    do(s.dma_start(T.WB[:, :], T.w[:, :]), e_w, 16)
    for k in range(8):
        do((s if k % 2 else sy).dma_start(T.BGL[16 * k:16 * k + 16, :], T.bag[:, fcol:fcol + 12]), e_bag, 16)

    e_ip, e_tr, e_trf, e_f = ev(), ev(), ev(), ev()
    do(g.iota(T.IP[:, :], [[0, 2]], 0, 1), e_ip)
    do(g.iota(T.CI[:, :], [[1, 7], [0, 2]], 0, 0), e_ip)
    do(g.iota(T.TR[:, :], [[16, 14]], B, 1), e_tr)
    do(g.iota(T.TRF[:, :], [[0, 4], [16, 3]], B, 1), e_trf)
    do(g.iota(T.F[:, :], [[0, FW]], 0, 0, allow_small_or_imprecise_dtypes=True), e_f)
    e_z, e_h0, e_h1, e_co = ev(), ev(), ev(), ev()
    do(v.memset(T.EB[:, 0:PAD], 0.0), e_z)
    do(v.memset(T.X[:, 0:B], -1.0 - OFFSET), e_z)
    wait("v", v, e_ip)
    do(v.tensor_scalar(T.PI[:, :], T.IP[:, :], 8, None, Op.bitwise_and), e_h0)
    wait("v", v, e_h0)
    do(v.tensor_scalar(T.PF32[:, :], T.PI[:, :], 0.875, None, Op.mult), e_h1)
    wait("v", v, e_h1)
    do(v.tensor_scalar(T.CO[:, :], T.CI[:, :], T.PF32[:, 0:1], None, Op.add), e_co)

    e1, e2, e3, e4, e5, e6 = ev(), ev(), ev(), ev(), ev(), ev()
    e_sc, e_val, e_e = ev(), ev(), ev()
    wait("v", v, e_ob)
    do(v.tensor_scalar(T.LO[:, :], T.OBL[:, :], 0x3FF, None, Op.bitwise_and), e1)
    wait("v", v, e_uv, e_z, e_co)
    do(v.tensor_scalar(T.SC[:, :], T.UVL[:, 0:14].indirect(T.CO[:, 0:14]), -OFFSET, None, Op.add), e_sc)
    wait("v", v, e1, e_tr)
    do(v.tensor_tensor(T.OFM[:, :], T.LO[:, :], T.TR[:, :], Op.min), e4)
    wait("v", v, e_sc)
    do(v.transpose(T.VAL[:, :], T.SC[:, :]), e_val)
    wait("v", v, e4)
    do(v.tensor_copy(T.OFS[:, 0:14:2], T.OFM[:, 0:7]), e5)
    do(v.tensor_copy(T.OFS[:, 1:14:2], T.OFM[:, 7:14]), e5)
    wait("v", v, e_val, e5)
    do(v.tensor_copy(T.X[:, 0:XW].indirect(T.OFS[:, 0:14]), T.VAL[:, :]), e6)
    e_fuv = [ev() for t in range(4)]
    wait("v", v, e_fl)
    for t in range(4):
        do(v.tensor_scalar(T["FUV%d" % t][:, :], T.FL[:, :], 4, PAD + t, Op.mult, Op.add), e_fuv[t])
    wait("v", v, e6)
    for t in range(4):
        do(v.tensor_scalar(T.E[:, :, t, :], T.X[:, 0:B], 4, 4 * OFFSET + PAD + t, Op.mult, Op.add), e_e)

    e_tu, e_tv = [ev() for a in range(4)], [ev() for a in range(4)]
    wait("sy", sy, e_e)
    for a in range(4):
        do(sy.dma_start(T.LUV[:, 128 * a:128 * a + 64], T.E[32 * a:32 * a + 8, :, :, :]), e_tu[a], 16)
        do(sy.dma_start(T.LUV[:, 128 * a + 64:128 * a + 128], T.E[32 * a + 8:32 * a + 16, :, :, :]), e_tv[a], 16)

    e_uf = [ev() for t in range(4)]
    wait("s", s, e_ex, e_z)
    for t in range(4):
        wait("s", s, e_fuv[t])
        do(s.activation(T.UF[:, 192 * t:192 * t + 192], T.EB[:, 0:WIN].indirect(T["FUV%d" % t][:, 0:12]), Copy), e_uf[t])
    wait("v", v, e_ex)
    e_hf, e_qf, e_qw = ev(), ev(), ev()
    e_b1, e_b2, e_lb = ev(), ev(), ev()
    for t in range(4):
        wait("v", v, e_uf[t])
        do(v.tensor_tensor(T.HF[:, t:768:4], T.EB[:, 0:WIN].indirect(T["FUV%d" % t][:, 12:24]),
                           T.UF[:, 192 * t:192 * t + 192], Op.add), e_hf)
        if t == 1:
            wait("v", v, e_bag)
            do(v.tensor_scalar(T.B1[:, :], T.BGL[:, :], 0x3FF, None, Op.bitwise_and), e_b1)
        if t == 2:
            wait("v", v, e_b1, e_trf)
            do(v.tensor_tensor(T.B2[:, :], T.B1[:, :], T.TRF[:, :], Op.min), e_b2)
    wait("v", v, e_b2)
    for o in range(NB):
        do(v.tensor_scalar(T.LB[:, :, 3 * o:3 * o + 3], T.B2[:, :], FS * o, None, Op.add), e_lb)
    wait("v", v, e_hf)
    do(v.quantize_mx(T.QF[:, 0:192], T.SF[:, 0:192], T.HF[:, 0:768]), e_qf)
    wait("v", v, e_w)
    do(v.quantize_mx(T.QW[:, 0:384], T.SW[:, 0:384], T.WB[:, 0:1536]), e_qw)

    e_q, e_h = [ev() for a in range(4)], [ev() for a in range(4)]

    def picked(a, second_item, lo, hi):
        c0 = 128 * a + 64 * second_item
        return T.EB[:, 0:WIN].indirect(T.LUV[:, c0 + lo // 4:c0 + hi // 4])

    def first(a, lo, hi, e):
        wait("s", s, e_tu[a])
        do(s.activation(T["UB%d" % a][:, 4 * lo:4 * hi], picked(a, 0, lo, hi), Copy), e)

    def second(a, lo, hi, e):
        wait("v", v, e_tv[a], e)
        do(v.tensor_tensor(T["HB%d" % a][:, 4 * lo:4 * hi], picked(a, 1, lo, hi), T["UB%d" % a][:, 4 * lo:4 * hi],
                           Op.add), e_h[a])

    def pack(a, *es):
        wait("v", v, e_h[a], *es)
        do(v.quantize_mx(T["Q%d" % a][:, 0:256], T["S%d" % a][:, 0:256], T["HB%d" % a][:, 0:1024]), e_q[a])

    for a in range(3):
        for lo, hi in zip(CUTS[a], CUTS[a][1:]):
            e = ev()
            first(a, lo, hi, e)
            second(a, lo, hi, e)
            if a and lo == 0:
                pack(a - 1)

    wait("te", te, e_qw)
    te.wait_ge(T.sem.farin, 4 * 2 * 2)
    e_pf, e_yf = [ev() for o in range(NB)], ev()
    for o in range(NB):
        do(te.matmul_mx(T.PFAR[:, 512 * o:512 * o + 192], T.QW[:, 128 * o:128 * o + 128], T.SW[:, 128 * o:128 * o + 128],
                        T.RF[:, 0:192], T.RFS[:, 0:192], True, True), e_pf[o])
    for o in range(NB):
        wait("s", s, e_pf[o])
        do(s.activation(T.YF[:, :, 48 * o:48 * o + 48], T.PFAR[:, 512 * o:512 * o + 192], Copy), e_yf)
    e_u3 = [ev(), ev(), ev()]
    first(3, 0, 128, e_u3[0])
    wait("s", s, e_tv[3])
    do(s.activation(T.VB[:, 256:512], picked(3, 1, 64, 128), Copy), e_u3[1])
    first(3, 128, 256, e_u3[2])
    do(s.activation(T.VB[:, 512:1024], picked(3, 1, 128, 256), Copy), e_u3[2])

    wait("v", v, e_lb, e_f)
    e_sum, e_put = [ev() for k in range(4)], [ev() for k in range(4)]

    def there(k):
        return T.F[:, 0:FW].indirect(T.LB[:, k, 0:9])

    def add(k):
        wait("v", v, e_put[k - 1])
        do(v.tensor_tensor(T.TMP[:, 144 * k:144 * k + 144], there(k), T.YF[:, k, :], Op.add), e_sum[k])

    def put(k):
        wait("v", v, e_sum[k] if k else e_yf)
        do(v.tensor_copy(there(k), T.TMP[:, 144 * k:144 * k + 144] if k else T.YF[:, k, :]), e_put[k])

    def own(i):
        if i == 0:
            return second(3, 0, 64, e_u3[0])
        wait("v", v, e_u3[min(i, 2)])
        do(v.tensor_tensor(T.HB3[:, B * i:B * i + B], T.VB[:, B * i:B * i + B], T.UB3[:, B * i:B * i + B], Op.add), e_h[3])

    sent = 0
    wait("g", g, e_qf)
    mine = [r for r in range(N) if SIDE[r] == SIDE[me]].index(me)
    for src, dst, wd in (("QF", "RF", 0), ("SF", "RFS", 1)):
        tr = []
        for k, r in enumerate(far):
            rid, pid, _ = topo.addr(cores[r])
            en = topo.engines(core, cores[r])
            n = len(en) // 4
            m = sum(1 << x for x in en[n * k:n * k + n])
            sv, dv = T[src][:, 48 * k:48 * k + 48], T[dst][:, 48 * mine:48 * mine + 48]
            if wd == 0:
                sv, dv = sv.bitcast(dt.uint8), dv.bitcast(dt.uint8)
            tr.append(RemoteDMATransfer(dst_ids=[DstId(rid=rid, pnc=pid)], dma_engine_mask=m, remote_sem=T.sem.farin,
                                        srcs=[sv], dsts=[dv]))
            sent += n
        g.remote_dma_fused(tr, local_sem=T.sem.sent)

    put(0)
    pack(2)
    arrived = []
    for a in range(3):
        r = order[a]
        rid, pid, _ = topo.addr(cores[r])
        en = topo.engines(core, cores[r])[-8:]
        m = sum(1 << x for x in en)
        wait("g", g, e_q[a])
        g.remote_dma(T["R%d" % a][:, 0:256].bitcast(dt.uint8), T["Q%d" % a][:, 0:256].bitcast(dt.uint8),
                     T.sem["in%d" % a], T.sem.sent, pid, rid, m)
        g.remote_dma(T["RS%d" % a][:, 0:256], T["S%d" % a][:, 0:256], T.sem["in%d" % a], T.sem.sent, pid, rid, m)
        sent += 2 * len(en)
        arrived.append(2 * len(en))

    add(1)
    own(0)
    put(1)
    own(1)
    add(2)
    own(2)
    put(2)
    own(3)
    add(3)
    pack(3)
    put(3)

    e_pn = [ev() for o in range(NB)]
    for i, a in enumerate((0, 2, 1, 3)):
        if a == 3:
            wait("te", te, e_q[3])
            qt, st = T.Q3, T.S3
        else:
            te.wait_ge(T.sem["in%d" % a], arrived[a])
            qt, st = T["R%d" % a], T["RS%d" % a]
        for o in range(NB):
            inst = te.matmul_mx(T.PN[:, 512 * o:512 * o + 256], T.QW[:, 128 * o:128 * o + 128],
                                T.SW[:, 128 * o:128 * o + 128], qt[:, 0:256], st[:, 0:256], i == 0, i == 3)
            if i == 3:
                do(inst, e_pn[o])

    wait("v", v, e_put[3])
    e_y = ev()
    for o in range(NB):
        e = ev()
        wait("v", v, e_pn[o])
        for i in range(4):
            do(v.tensor_tensor(T.YO[:, B * o + 64 * i:B * o + 64 * i + 64], T.PN[:, 512 * o + i:512 * o + B:4],
                               T.F[:, FS * o + 64 * i:FS * o + 64 * i + 64], Op.add), e)
        wait("sy", sy, e)
        do(sy.dma_start(T.y[:, B * o:B * o + B], T.YO[:, B * o:B * o + B]), e_y, 16)
    wait("sy", sy, e_y)
    g.wait_ge(T.sem.sent, sent)
